import numpy as np
import ml_dtypes


def mxq(x, axis, fmt="e4m3"):
    dtype, down = {"e4m3": (ml_dtypes.float8_e4m3fn, 7), "e5m2": (ml_dtypes.float8_e5m2, 14)}[fmt]
    v = np.moveaxis(np.asarray(x, np.float32).astype(ml_dtypes.bfloat16).astype(np.float64), axis, -1)
    blocks = v.reshape(v.shape[:-1] + (-1, 32))
    amax = np.abs(blocks).max(-1, keepdims=True)
    byte = np.maximum(np.where(amax > 0, np.frexp(amax)[1] - 1 + 127, 0) - down, 1)
    scale = np.exp2(byte - 127.0)
    codes = (blocks / scale).astype(np.float32).astype(dtype).astype(np.float64)
    return np.moveaxis((codes * scale).reshape(v.shape), -1, axis)


WIDE = False


def mx_kscale(k):
    if not WIDE:
        return np.ones(k)
    levels = np.array([10, -10, 5, -5, 0])
    if k % 512:
        return np.exp2(np.random.permutation(np.resize(levels, k // 32))).repeat(32)
    a = np.empty((k // 512, 16))
    for p in range(k // 512):
        a[p, :8] = np.random.permutation(np.resize(levels, 8))
        for g in range(8):
            far = levels[np.abs(levels - a[p, g]) >= 10]
            a[p, g + 8] = far[np.random.randint(len(far))]
    return np.exp2(a.ravel()).repeat(32)


def f64(x):
    return np.asarray(x).astype(np.float64)


def striped8(idx):
    return np.asarray(idx).reshape(8, -1, 16).transpose(0, 2, 1).reshape(128, -1).astype(np.uint16)


def unstriped8(offs):
    return offs.reshape(8, 16, -1).transpose(0, 2, 1).reshape(8, -1).astype(np.int64)


def pick8(x, idx, run):
    r = np.arange(len(x))
    return x[r[:, None], idx[r % (8 * run) // run]]


E2M1 = np.array([0.0, 0.5, 1.0, 1.5, 2.0, 3.0, 4.0, 6.0, -0.0, -0.5, -1.0, -1.5, -2.0, -3.0, -4.0, -6.0])


def pack_weight(w, fmt):
    k, n = w.shape
    w = f64(np.asarray(w, np.float32).astype(ml_dtypes.bfloat16)).reshape(k // 32, 32, n)
    amax = np.abs(w).max(1)
    if fmt == "e4m3":
        byte = np.frexp(amax)[1] - 1 + 127 - 7
    else:
        mant, ex = np.frexp(amax / 6.0)
        byte = np.where(mant > 0.5, ex, ex - 1) + 127
    byte = np.clip(np.where(amax > 0, byte, 1), 1, 254)
    scaled = (w * np.exp2(127.0 - byte)[:, None, :]).reshape(k, n).astype(np.float32)
    by_word = np.ascontiguousarray(scaled.reshape(k // 512, 128, 4, n).transpose(0, 1, 3, 2))
    if fmt == "e4m3":
        words = by_word.astype(ml_dtypes.float8_e4m3fn).view(np.uint8)
    else:
        c = by_word.astype(ml_dtypes.float4_e2m1fn).view(np.uint8) & 0xF
        words = (c[..., 0::2] | (c[..., 1::2] << 4)).reshape(k // 512, 128, 2 * n)
    return np.ascontiguousarray(words), np.ascontiguousarray(byte.astype(np.uint8).reshape(k // 512, 16, n))


def unpack_weight(words, scales, fmt):
    g, _, n = scales.shape
    words = np.ascontiguousarray(words).reshape(g, 128, n, -1)
    if fmt == "e4m3":
        vals = words.view(ml_dtypes.float8_e4m3fn).astype(np.float64)
    else:
        nib = np.empty((g, 128, n, 4), np.uint8)
        nib[..., 0::2] = words & 0xF
        nib[..., 1::2] = words >> 4
        vals = E2M1[nib]
    vals = vals * np.repeat(np.exp2(scales.astype(np.float64) - 127.0), 8, axis=1)[..., None]
    return vals.transpose(0, 1, 3, 2).reshape(g * 512, n)


D, T, U, I, Q = 512, 1024, 1024, 512, 128


def setup_inputs():
    n = np.random.standard_normal
    idx = np.stack([np.random.permutation(T)[:I] for _ in range(8)])
    idx2 = np.stack([np.random.permutation(I)[:I] for _ in range(8)])
    idx3 = np.stack([np.random.permutation(U)[:I] for _ in range(8)])
    idx4 = np.stack([np.random.permutation(U)[:I] for _ in range(8)])
    fd = mx_kscale(D)
    keysp = pack_weight(n((D, T)) / fd[:, None], "e2m1")
    notesp = pack_weight(n((D, U)) / fd[:, None], "e4m3")
    return {
        "query": (n((D, Q)) * 1.0 / np.sqrt(D) * fd[:, None]).astype(np.float32),
        "keys_words": keysp[0],
        "keys_scales": keysp[1],
        "notes_words": notesp[0],
        "notes_scales": notesp[1],
        "offs": striped8(idx),
        "offs2": striped8(idx2),
        "offs3": striped8(idx3),
        "offs4": striped8(idx4),
    }


def reference(query, keys_words, keys_scales, notes_words, notes_scales, offs, offs2, offs3, offs4):
    idx = unstriped8(offs)
    idx2 = unstriped8(offs2)
    idx3 = unstriped8(offs3)
    idx4 = unstriped8(offs4)
    keysu = unpack_weight(keys_words, keys_scales, "e2m1")
    notesu = unpack_weight(notes_words, notes_scales, "e4m3")
    queryq = mxq(f64(query), 0, "e4m3")
    a = queryq.T @ keysu
    b = queryq.T @ notesu
    w = pick8(a, idx, 16) * 1.5
    v = pick8(w, idx2, 16)
    r = w - v
    f1 = np.zeros((Q, U))
    f1[np.arange(Q)[:, None], idx3[np.arange(Q) % 128 // 16]] = r
    bb = b + f1
    y = np.maximum(pick8(bb, idx4, 16), v)
    return y

@@ -1,0 +1,132 @@
+from contextlib import ExitStack
+
+import concourse.mybir as mybir
+
+D, T, U, I, Q = 512, 1024, 1024, 512, 128
+FLOPS = 2 * D * Q * (T + U)
+
+F32 = mybir.dt.float32
+BF16 = mybir.dt.bfloat16
+I32 = mybir.dt.int32
+U32 = mybir.dt.uint32
+U16 = mybir.dt.uint16
+U8 = mybir.dt.uint8
+FP8X4 = mybir.dt.float8_e4m3fn_x4
+FP4X4 = mybir.dt.float4_e2m1fn_x4
+ALU = mybir.AluOpType
+COPY = mybir.ActivationFunctionType.Copy
+
+P = 128
+PACK = 4
+LIST_COLS = I // 16
+HALF = I // 2
+A_PIECES = (256, 256, 256, 128, 128)
+BANK = 512
+
+
+def tile_attend_slotshuffle_two_kernel(tc, query, keys_words, keys_scales, notes_words, notes_scales, offs, offs2, offs3, offs4, out):
+    nc = tc.nc
+    with ExitStack() as ctx:
+        sb = ctx.enter_context(tc.tile_pool(name="sb", bufs=1))
+        psum = ctx.enter_context(tc.psum_pool(name="psum", bufs=1))
+
+        q_raw = sb.tile([P, PACK, Q], F32, name="q_raw")
+        k_words = sb.tile([P, 2 * T], U8, name="k_words", align_bytes=64)
+        k_scales = sb.tile([P, T], U8, name="k_scales", align_bytes=64)
+        n_words = sb.tile([P, U], U32, name="n_words", align_bytes=64)
+        n_scales = sb.tile([P, U], U8, name="n_scales", align_bytes=64)
+        list_a = sb.tile([P, LIST_COLS], U16, name="list_a")
+        list_w = sb.tile([P, LIST_COLS], U16, name="list_w")
+        list_f = sb.tile([P, LIST_COLS], U16, name="list_f")
+        list_b = sb.tile([P, LIST_COLS], U16, name="list_b")
+        f1 = sb.tile([P, U], F32, name="f1")
+
+        nc.vector.memset(k_scales[:].bitcast(I32), 0)
+        nc.vector.memset(n_scales[:].bitcast(I32), 0)
+        nc.vector.memset(f1[:], 0.0)
+
+        nc.sync.dma_start(out=q_raw[:], in_=query.rearrange("(p j) q -> p j q", j=PACK))
+        nc.sync.dma_start(out=k_words[:].bitcast(I32), in_=keys_words[0].bitcast(I32))
+        for quad in range(4):
+            nc.scalar.dma_start(
+                out=k_scales[32 * quad : 32 * quad + 4, :].bitcast(I32),
+                in_=keys_scales[0, 4 * quad : 4 * quad + 4, :].bitcast(I32),
+            )
+        nc.sync.dma_start(list_a[:], offs)
+        nc.sync.dma_start(list_w[:], offs2)
+        nc.sync.dma_start(out=n_words[:].bitcast(I32), in_=notes_words[0].rearrange("p n t -> p (n t)").bitcast(I32))
+        nc.sync.dma_start(list_f[:], offs3)
+        for quad in range(4):
+            nc.sync.dma_start(
+                out=n_scales[32 * quad : 32 * quad + 4, :].bitcast(I32),
+                in_=notes_scales[0, 4 * quad : 4 * quad + 4, :].bitcast(I32),
+            )
+        nc.sync.dma_start(list_b[:], offs4)
+
+        q_bf = sb.tile([P, Q, PACK], BF16, name="q_bf", align_bytes=64)
+        nc.vector.tensor_copy(
+            out=q_bf[:].rearrange("p (c i) j -> p c j i", i=4),
+            in_=q_raw[:].rearrange("p j (c i) -> p c j i", i=4),
+        )
+        q_codes = sb.tile([P, Q], U32, name="q_codes", align_bytes=64)
+        q_scales = sb.tile([P, Q], U8, name="q_scales", align_bytes=64)
+        nc.vector.quantize_mx(out=q_codes[:].bitcast(FP8X4), scales=q_scales[:], in_=q_bf[:].rearrange("p q j -> p (q j)"))
+
+        a = sb.tile([P, T], F32, name="a")
+        col = 0
+        for piece, width in enumerate(A_PIECES):
+            acc = psum.tile([P, width], F32, name="a_acc%d" % piece)
+            nc.tensor.matmul_mx(
+                out=acc[:],
+                lhsT=q_codes[:].bitcast(FP8X4),
+                lhsT_scale=q_scales[:],
+                rhs=k_words[:, 2 * col : 2 * (col + width)].bitcast(FP4X4),
+                rhs_scale=k_scales[:, col : col + width],
+                start=True,
+                stop=True,
+            )
+            if piece % 2 == 0:
+                nc.vector.tensor_copy(out=a[:, col : col + width], in_=acc[:])
+            else:
+                nc.scalar.activation(out=a[:, col : col + width], in_=acc[:], func=COPY)
+            col = col + width
+
+        b_acc = []
+        for bank in range(U // BANK):
+            acc = psum.tile([P, BANK], F32, name="b_acc%d" % bank)
+            nc.tensor.matmul_mx(
+                out=acc[:],
+                lhsT=q_codes[:].bitcast(FP8X4),
+                lhsT_scale=q_scales[:],
+                rhs=n_words[:, bank * BANK : (bank + 1) * BANK].bitcast(FP8X4),
+                rhs_scale=n_scales[:, bank * BANK : (bank + 1) * BANK],
+                start=True,
+                stop=True,
+            )
+            b_acc.append(acc)
+
+        half_cols = LIST_COLS // 2
+        w = sb.tile([P, I], F32, name="w")
+        nc.vector.tensor_scalar(w[:, :HALF], a[:].indirect(list_a[:, :half_cols]), 1.5, 0.0, ALU.mult, ALU.add)
+        nc.scalar.activation(out=w[:, HALF:], in_=a[:].indirect(list_a[:, half_cols:]), func=COPY, scale=1.5)
+
+        neg_v = sb.tile([P, I], F32, name="neg_v")
+        nc.vector.tensor_scalar(neg_v[:, :HALF], w[:].indirect(list_w[:, :half_cols]), -1.0, 0.0, ALU.mult, ALU.add)
+        nc.scalar.activation(out=neg_v[:, HALF:], in_=w[:].indirect(list_w[:, half_cols:]), func=COPY, scale=-1.0)
+
+        nc.vector.tensor_tensor(f1[:].indirect(list_f[:]), w[:], neg_v[:], ALU.add)
+
+        bb = sb.tile([P, U], F32, name="bb")
+        for bank in range(U // BANK):
+            cols = slice(bank * BANK, (bank + 1) * BANK)
+            nc.vector.tensor_tensor(bb[:, cols], b_acc[bank][:], f1[:, cols], ALU.add)
+
+        picked = sb.tile([P, I], F32, name="picked")
+        nc.vector.tensor_copy(picked[:, :HALF], bb[:].indirect(list_b[:, :half_cols]))
+        nc.scalar.activation(out=picked[:, HALF:], in_=bb[:].indirect(list_b[:, half_cols:]), func=COPY)
+
+        res = sb.tile([P, I], F32, name="res")
+        for half in range(2):
+            cols = slice(half * HALF, (half + 1) * HALF)
+            nc.vector.scalar_tensor_tensor(res[:, cols], neg_v[:, cols], -1.0, picked[:, cols], ALU.mult, ALU.max)
+            nc.sync.dma_start(out=out[:, cols], in_=res[:, cols])

@@ -22,6 +22,7 @@ LIST_COLS = I // 16
 HALF = I // 2
 A_PIECES = (256, 256, 256, 128, 128)
 BANK = 512
+POOL_COLS = 192
 
 
 def tile_attend_slotshuffle_two_kernel(tc, query, keys_words, keys_scales, notes_words, notes_scales, offs, offs2, offs3, offs4, out):
@@ -31,7 +32,7 @@ def tile_attend_slotshuffle_two_kernel(tc, query, keys_words, keys_scales, notes
         psum = ctx.enter_context(tc.psum_pool(name="psum", bufs=1))
 
         q_raw = sb.tile([P, PACK, Q], F32, name="q_raw")
-        k_words = sb.tile([P, 2 * T], U8, name="k_words", align_bytes=64)
+        k_words = [sb.tile([P, T], U8, name="k_words%d" % half, align_bytes=64) for half in range(2)]
         k_scales = sb.tile([P, T], U8, name="k_scales", align_bytes=64)
         n_words = sb.tile([P, U], U32, name="n_words", align_bytes=64)
         n_scales = sb.tile([P, U], U8, name="n_scales", align_bytes=64)
@@ -46,7 +47,8 @@ def tile_attend_slotshuffle_two_kernel(tc, query, keys_words, keys_scales, notes
         nc.vector.memset(f1[:], 0.0)
 
         nc.sync.dma_start(out=q_raw[:], in_=query.rearrange("(p j) q -> p j q", j=PACK))
-        nc.sync.dma_start(out=k_words[:].bitcast(I32), in_=keys_words[0].bitcast(I32))
+        for half in range(2):
+            nc.sync.dma_start(out=k_words[half][:].bitcast(I32), in_=keys_words[0, :, half * T : (half + 1) * T].bitcast(I32))
         for quad in range(4):
             nc.scalar.dma_start(
                 out=k_scales[32 * quad : 32 * quad + 4, :].bitcast(I32),
@@ -64,13 +66,21 @@ def tile_attend_slotshuffle_two_kernel(tc, query, keys_words, keys_scales, notes
         nc.sync.dma_start(list_b[:], offs4)
 
         q_bf = sb.tile([P, Q, PACK], BF16, name="q_bf", align_bytes=64)
-        nc.vector.tensor_copy(
-            out=q_bf[:].rearrange("p (c i) j -> p c j i", i=4),
-            in_=q_raw[:].rearrange("p j (c i) -> p c j i", i=4),
-        )
+        for part in range(2):
+            cols = slice(part * Q // 2, (part + 1) * Q // 2)
+            nc.vector.tensor_copy(
+                out=q_bf[:, cols, :].rearrange("p (c i) j -> p c j i", i=4),
+                in_=q_raw[:, :, cols].rearrange("p j (c i) -> p c j i", i=4),
+            )
         q_codes = sb.tile([P, Q], U32, name="q_codes", align_bytes=64)
         q_scales = sb.tile([P, Q], U8, name="q_scales", align_bytes=64)
-        nc.vector.quantize_mx(out=q_codes[:].bitcast(FP8X4), scales=q_scales[:], in_=q_bf[:].rearrange("p q j -> p (q j)"))
+        for part in range(2):
+            cols = slice(part * Q // 2, (part + 1) * Q // 2)
+            nc.vector.quantize_mx(
+                out=q_codes[:, cols].bitcast(FP8X4),
+                scales=q_scales[:, cols],
+                in_=q_bf[:, cols, :].rearrange("p q j -> p (q j)"),
+            )
 
         a = sb.tile([P, T], F32, name="a")
         col = 0
@@ -80,7 +90,7 @@ def tile_attend_slotshuffle_two_kernel(tc, query, keys_words, keys_scales, notes
                 out=acc[:],
                 lhsT=q_codes[:].bitcast(FP8X4),
                 lhsT_scale=q_scales[:],
-                rhs=k_words[:, 2 * col : 2 * (col + width)].bitcast(FP4X4),
+                rhs=k_words[col // BANK][:, 2 * (col % BANK) : 2 * (col % BANK + width)].bitcast(FP4X4),
                 rhs_scale=k_scales[:, col : col + width],
                 start=True,
                 stop=True,
@@ -117,9 +127,11 @@ def tile_attend_slotshuffle_two_kernel(tc, query, keys_words, keys_scales, notes
         nc.vector.tensor_tensor(f1[:].indirect(list_f[:]), w[:], neg_v[:], ALU.add)
 
         bb = sb.tile([P, U], F32, name="bb")
-        for bank in range(U // BANK):
-            cols = slice(bank * BANK, (bank + 1) * BANK)
-            nc.vector.tensor_tensor(bb[:, cols], b_acc[bank][:], f1[:, cols], ALU.add)
+        b_tail = sb.tile([P, POOL_COLS], F32, name="b_tail")
+        nc.scalar.activation(out=b_tail[:], in_=b_acc[1][:, BANK - POOL_COLS :], func=COPY)
+        nc.gpsimd.tensor_tensor(bb[:, U - POOL_COLS :], b_tail[:], f1[:, U - POOL_COLS :], ALU.add)
+        nc.vector.tensor_tensor(bb[:, :BANK], b_acc[0][:], f1[:, :BANK], ALU.add)
+        nc.vector.tensor_tensor(bb[:, BANK : U - POOL_COLS], b_acc[1][:, : BANK - POOL_COLS], f1[:, BANK : U - POOL_COLS], ALU.add)
 
         picked = sb.tile([P, I], F32, name="picked")
         nc.vector.tensor_copy(picked[:, :HALF], bb[:].indirect(list_b[:, :half_cols]))

@@ -22,7 +22,7 @@ LIST_COLS = I // 16
 HALF = I // 2
 A_PIECES = (256, 256, 256, 128, 128)
 BANK = 512
-POOL_COLS = 192
+POOL_COLS = 256
 
 
 def tile_attend_slotshuffle_two_kernel(tc, query, keys_words, keys_scales, notes_words, notes_scales, offs, offs2, offs3, offs4, out):

from contextlib import ExitStack

import concourse.mybir as mybir

D, T, U, I, Q = 512, 1024, 1024, 512, 128
FLOPS = 2 * D * Q * (T + U)

F32 = mybir.dt.float32
BF16 = mybir.dt.bfloat16
I32 = mybir.dt.int32
U32 = mybir.dt.uint32
U16 = mybir.dt.uint16
U8 = mybir.dt.uint8
FP8X4 = mybir.dt.float8_e4m3fn_x4
FP4X4 = mybir.dt.float4_e2m1fn_x4
ALU = mybir.AluOpType
COPY = mybir.ActivationFunctionType.Copy

P = 128
PACK = 4
LIST_COLS = I // 16
HALF = I // 2
A_PIECES = (256, 256, 256, 128, 128)
BANK = 512
POOL_COLS = 256


def tile_attend_slotshuffle_two_kernel(tc, query, keys_words, keys_scales, notes_words, notes_scales, offs, offs2, offs3, offs4, out):
    nc = tc.nc
    with ExitStack() as ctx:
        sb = ctx.enter_context(tc.tile_pool(name="sb", bufs=1))
        psum = ctx.enter_context(tc.psum_pool(name="psum", bufs=1))

        q_raw = sb.tile([P, PACK, Q], F32, name="q_raw")
        k_words = [sb.tile([P, T], U8, name="k_words%d" % half, align_bytes=64) for half in range(2)]
        k_scales = sb.tile([P, T], U8, name="k_scales", align_bytes=64)
        n_words = sb.tile([P, U], U32, name="n_words", align_bytes=64)
        n_scales = sb.tile([P, U], U8, name="n_scales", align_bytes=64)
        list_a = sb.tile([P, LIST_COLS], U16, name="list_a")
        list_w = sb.tile([P, LIST_COLS], U16, name="list_w")
        list_f = sb.tile([P, LIST_COLS], U16, name="list_f")
        list_b = sb.tile([P, LIST_COLS], U16, name="list_b")
        f1 = sb.tile([P, U], F32, name="f1")

        nc.vector.memset(k_scales[:].bitcast(I32), 0)
        nc.vector.memset(n_scales[:].bitcast(I32), 0)
        nc.vector.memset(f1[:], 0.0)

        nc.sync.dma_start(out=q_raw[:], in_=query.rearrange("(p j) q -> p j q", j=PACK))
        for half in range(2):
            nc.sync.dma_start(out=k_words[half][:].bitcast(I32), in_=keys_words[0, :, half * T : (half + 1) * T].bitcast(I32))
        for quad in range(4):
            nc.scalar.dma_start(
                out=k_scales[32 * quad : 32 * quad + 4, :].bitcast(I32),
                in_=keys_scales[0, 4 * quad : 4 * quad + 4, :].bitcast(I32),
            )
        nc.sync.dma_start(list_a[:], offs)
        nc.sync.dma_start(list_w[:], offs2)
        nc.sync.dma_start(out=n_words[:].bitcast(I32), in_=notes_words[0].rearrange("p n t -> p (n t)").bitcast(I32))
        nc.sync.dma_start(list_f[:], offs3)
        for quad in range(4):
            nc.sync.dma_start(
                out=n_scales[32 * quad : 32 * quad + 4, :].bitcast(I32),
                in_=notes_scales[0, 4 * quad : 4 * quad + 4, :].bitcast(I32),
            )
        nc.sync.dma_start(list_b[:], offs4)

        q_bf = sb.tile([P, Q, PACK], BF16, name="q_bf", align_bytes=64)
        for part in range(2):
            cols = slice(part * Q // 2, (part + 1) * Q // 2)
            nc.vector.tensor_copy(
                out=q_bf[:, cols, :].rearrange("p (c i) j -> p c j i", i=4),
                in_=q_raw[:, :, cols].rearrange("p j (c i) -> p c j i", i=4),
            )
        q_codes = sb.tile([P, Q], U32, name="q_codes", align_bytes=64)
        q_scales = sb.tile([P, Q], U8, name="q_scales", align_bytes=64)
        for part in range(2):
            cols = slice(part * Q // 2, (part + 1) * Q // 2)
            nc.vector.quantize_mx(
                out=q_codes[:, cols].bitcast(FP8X4),
                scales=q_scales[:, cols],
                in_=q_bf[:, cols, :].rearrange("p q j -> p (q j)"),
            )

        a = sb.tile([P, T], F32, name="a")
        col = 0
        for piece, width in enumerate(A_PIECES):
            acc = psum.tile([P, width], F32, name="a_acc%d" % piece)
            nc.tensor.matmul_mx(
                out=acc[:],
                lhsT=q_codes[:].bitcast(FP8X4),
                lhsT_scale=q_scales[:],
                rhs=k_words[col // BANK][:, 2 * (col % BANK) : 2 * (col % BANK + width)].bitcast(FP4X4),
                rhs_scale=k_scales[:, col : col + width],
                start=True,
                stop=True,
            )
            if piece % 2 == 0:
                nc.vector.tensor_copy(out=a[:, col : col + width], in_=acc[:])
            else:
                nc.scalar.activation(out=a[:, col : col + width], in_=acc[:], func=COPY)
            col = col + width

        b_acc = []
        for bank in range(U // BANK):
            acc = psum.tile([P, BANK], F32, name="b_acc%d" % bank)
            nc.tensor.matmul_mx(
                out=acc[:],
                lhsT=q_codes[:].bitcast(FP8X4),
                lhsT_scale=q_scales[:],
                rhs=n_words[:, bank * BANK : (bank + 1) * BANK].bitcast(FP8X4),
                rhs_scale=n_scales[:, bank * BANK : (bank + 1) * BANK],
                start=True,
                stop=True,
            )
            b_acc.append(acc)

        half_cols = LIST_COLS // 2
        w = sb.tile([P, I], F32, name="w")
        nc.vector.tensor_scalar(w[:, :HALF], a[:].indirect(list_a[:, :half_cols]), 1.5, 0.0, ALU.mult, ALU.add)
        nc.scalar.activation(out=w[:, HALF:], in_=a[:].indirect(list_a[:, half_cols:]), func=COPY, scale=1.5)

        neg_v = sb.tile([P, I], F32, name="neg_v")
        nc.vector.tensor_scalar(neg_v[:, :HALF], w[:].indirect(list_w[:, :half_cols]), -1.0, 0.0, ALU.mult, ALU.add)
        nc.scalar.activation(out=neg_v[:, HALF:], in_=w[:].indirect(list_w[:, half_cols:]), func=COPY, scale=-1.0)

        nc.vector.tensor_tensor(f1[:].indirect(list_f[:]), w[:], neg_v[:], ALU.add)

        bb = sb.tile([P, U], F32, name="bb")
        b_tail = sb.tile([P, POOL_COLS], F32, name="b_tail")
        nc.scalar.activation(out=b_tail[:], in_=b_acc[1][:, BANK - POOL_COLS :], func=COPY)
        nc.gpsimd.tensor_tensor(bb[:, U - POOL_COLS :], b_tail[:], f1[:, U - POOL_COLS :], ALU.add)
        nc.vector.tensor_tensor(bb[:, :BANK], b_acc[0][:], f1[:, :BANK], ALU.add)
        nc.vector.tensor_tensor(bb[:, BANK : U - POOL_COLS], b_acc[1][:, : BANK - POOL_COLS], f1[:, BANK : U - POOL_COLS], ALU.add)

        picked = sb.tile([P, I], F32, name="picked")
        nc.vector.tensor_copy(picked[:, :HALF], bb[:].indirect(list_b[:, :half_cols]))
        nc.scalar.activation(out=picked[:, HALF:], in_=bb[:].indirect(list_b[:, half_cols:]), func=COPY)

        res = sb.tile([P, I], F32, name="res")
        for half in range(2):
            cols = slice(half * HALF, (half + 1) * HALF)
            nc.vector.scalar_tensor_tensor(res[:, cols], neg_v[:, cols], -1.0, picked[:, cols], ALU.mult, ALU.max)
            nc.sync.dma_start(out=out[:, cols], in_=res[:, cols])
